import numpy as np
import ml_dtypes


def mxq(x, axis, fmt="e4m3"):
    dtype, down = {"e4m3": (ml_dtypes.float8_e4m3fn, 7), "e5m2": (ml_dtypes.float8_e5m2, 14)}[fmt]
    v = np.moveaxis(np.asarray(x, np.float32).astype(ml_dtypes.bfloat16).astype(np.float64), axis, -1)
    blocks = v.reshape(v.shape[:-1] + (-1, 32))
    amax = np.abs(blocks).max(-1, keepdims=True)
    byte = np.maximum(np.where(amax > 0, np.frexp(amax)[1] - 1 + 127, 0) - down, 1)
    scale = np.exp2(byte - 127.0)
    codes = (blocks / scale).astype(np.float32).astype(dtype).astype(np.float64)
    return np.moveaxis((codes * scale).reshape(v.shape), -1, axis)


WIDE = False


def mx_kscale(k):
    if not WIDE:
        return np.ones(k)
    levels = np.array([10, -10, 5, -5, 0])
    if k % 512:
        return np.exp2(np.random.permutation(np.resize(levels, k // 32))).repeat(32)
    a = np.empty((k // 512, 16))
    for p in range(k // 512):
        a[p, :8] = np.random.permutation(np.resize(levels, 8))
        for g in range(8):
            far = levels[np.abs(levels - a[p, g]) >= 10]
            a[p, g + 8] = far[np.random.randint(len(far))]
    return np.exp2(a.ravel()).repeat(32)


def f64(x):
    return np.asarray(x).astype(np.float64)


def striped(idx):
    return np.tile(idx.reshape(-1, 16).T, (8, 1)).astype(np.uint16)


def unstriped(offs):
    return offs[:16].T.reshape(-1).astype(np.int64)


E2M1 = np.array([0.0, 0.5, 1.0, 1.5, 2.0, 3.0, 4.0, 6.0, -0.0, -0.5, -1.0, -1.5, -2.0, -3.0, -4.0, -6.0])


def pack_weight(w, fmt):
    k, n = w.shape
    w = f64(np.asarray(w, np.float32).astype(ml_dtypes.bfloat16)).reshape(k // 32, 32, n)
    amax = np.abs(w).max(1)
    if fmt == "e4m3":
        byte = np.frexp(amax)[1] - 1 + 127 - 7
    else:
        mant, ex = np.frexp(amax / 6.0)
        byte = np.where(mant > 0.5, ex, ex - 1) + 127
    byte = np.clip(np.where(amax > 0, byte, 1), 1, 254)
    scaled = (w * np.exp2(127.0 - byte)[:, None, :]).reshape(k, n).astype(np.float32)
    by_word = np.ascontiguousarray(scaled.reshape(k // 512, 128, 4, n).transpose(0, 1, 3, 2))
    if fmt == "e4m3":
        words = by_word.astype(ml_dtypes.float8_e4m3fn).view(np.uint8)
    else:
        c = by_word.astype(ml_dtypes.float4_e2m1fn).view(np.uint8) & 0xF
        words = (c[..., 0::2] | (c[..., 1::2] << 4)).reshape(k // 512, 128, 2 * n)
    return np.ascontiguousarray(words), np.ascontiguousarray(byte.astype(np.uint8).reshape(k // 512, 16, n))


def unpack_weight(words, scales, fmt):
    g, _, n = scales.shape
    words = np.ascontiguousarray(words).reshape(g, 128, n, -1)
    if fmt == "e4m3":
        vals = words.view(ml_dtypes.float8_e4m3fn).astype(np.float64)
    else:
        nib = np.empty((g, 128, n, 4), np.uint8)
        nib[..., 0::2] = words & 0xF
        nib[..., 1::2] = words >> 4
        vals = E2M1[nib]
    vals = vals * np.repeat(np.exp2(scales.astype(np.float64) - 127.0), 8, axis=1)[..., None]
    return vals.transpose(0, 1, 3, 2).reshape(g * 512, n)


K, T, E, C, N = 1024, 640, 15, 128, 256
TOP = 3


def by_expert(wq, xq):
    return np.concatenate([wq[e].T @ xq[:, e * C:(e + 1) * C] for e in range(E)], axis=1)


def setup_inputs():
    n = np.random.standard_normal
    s = mx_kscale(K)[:, None]
    deal = np.repeat(np.arange(E), C).reshape(TOP, T)[:, np.random.permutation(T)]
    deal = np.take_along_axis(deal, np.argsort(np.random.rand(TOP, T), axis=0), axis=0)
    for _ in range(8):
        s_, t_ = np.random.permutation(T).reshape(2, -1); r = np.random.randint(TOP, size=T // 2); x, y = deal[r, s_].copy(), deal[r, t_].copy()
        ok = ~((deal[:, s_] == y).any(0) | (deal[:, t_] == x).any(0)); deal[r[ok], s_[ok]] = y[ok]; deal[r[ok], t_[ok]] = x[ok]
    order = np.lexsort((np.random.rand(TOP * T), deal.reshape(-1)))
    slot_token = order % T; pos = np.empty(TOP * T, np.int64); pos[order] = np.arange(TOP * T); pos = pos.reshape(TOP, T)
    g = np.random.uniform(0.5, 1.5, (TOP, T)); g = g / g.sum(0)
    x = pack_weight(n((K, T)) * s, "e4m3")
    return {
        "x_words": x[0],
        "x_scales": x[1],
        "w": (n((E, K, N)) / np.sqrt(K) / s[None]).astype(np.float32),
        "b": (0.3 * n((N, E))).astype(np.float32),
        "gate": np.stack([np.tile(r, (N, 1)) for r in g]).astype(np.float32),
        "offs": striped(slot_token),
        "pos1": striped(pos[0]),
        "pos2": striped(pos[1]),
        "pos3": striped(pos[2]),
    }


def reference(x_words, x_scales, w, b, gate, offs, pos1, pos2, pos3):
    idx = unstriped(offs)
    xq = unpack_weight(x_words, x_scales, "e4m3")[:, idx]
    y = by_expert(mxq(f64(w), 1, "e4m3"), xq)
    y = y + np.repeat(f64(b), C, axis=1)
    return sum(f64(gate[r]) * y[:, unstriped(p)] for r, p in enumerate((pos1, pos2, pos3)))

@@ -1,0 +1,263 @@
+from contextlib import ExitStack
+
+import concourse.mybir as mybir
+
+K, T, E, C, N = 1024, 640, 15, 128, 256
+TOP = 3
+S = E * C
+FLOPS = 2 * K * N * S
+
+F32 = mybir.dt.float32
+BF16 = mybir.dt.bfloat16
+I32 = mybir.dt.int32
+U32 = mybir.dt.uint32
+U16 = mybir.dt.uint16
+U8 = mybir.dt.uint8
+FP8X4 = mybir.dt.float8_e4m3fn_x4
+IDENT = mybir.ActivationFunctionType.Identity
+MULT = mybir.AluOpType.mult
+ADD = mybir.AluOpType.add
+
+P = 128
+PACK = 4
+PASSES = K // (P * PACK)
+HALVES = N // P
+SPLIT = 5
+WHOLE = E - SPLIT
+GROUP = 3
+VEC_WHOLE = 64
+VEC_HALF = 32
+FIRST_OUT = 384
+SUM_HOSTS = ((E - 2, 1, 1), (E - 1, 1, 1))
+STARTS = ((0, 3, 6, 9, 12), (0, 1, 4, 7, 10, 13), (0, 2, 5, 8, 11, 14))
+
+
+def tile_moe_pkd_lin_bias_kernel(
+    tc, x_words, x_scales, w, b, gate, offs, pos1, pos2, pos3, out
+):
+    nc = tc.nc
+    with ExitStack() as ctx:
+        keep = ctx.enter_context(tc.tile_pool(name="keep", bufs=1))
+        ring = ctx.enter_context(tc.tile_pool(name="ring", bufs=4))
+        ring_half = ctx.enter_context(tc.tile_pool(name="ring_half", bufs=6))
+        ring_tok = ctx.enter_context(tc.tile_pool(name="ring_tok", bufs=2))
+        psum = ctx.enter_context(tc.psum_pool(name="psum", bufs=8))
+
+        offs_sb = keep.tile([P, S // 16], U16, name="offs_sb")
+        pos_sb = [keep.tile([P, T // 16], U16, name=f"pos_sb{r}") for r in range(TOP)]
+        xw = keep.tile([P, PASSES * T], I32, name="xw", align_bytes=64)
+        xs = keep.tile([P, T // 4], I32, name="xs", align_bytes=64)
+        bias = keep.tile([P, HALVES, E], F32, name="bias")
+        gates = [[keep.tile([P, T], F32, name=f"gate{h}{r}") for r in range(TOP)] for h in range(HALVES)]
+        y = [keep.tile([P, S], F32, name=f"y{h}") for h in range(HALVES)]
+        raw = {}
+        hosts = {}
+
+        def load_whole(e, o):
+            if o is None:
+                t = keep.tile([P, PASSES, PACK, N], F32, name=f"raw{e}")
+                nc.sync.dma_start(
+                    out=t[:].rearrange("p o j n -> p o (j n)"),
+                    in_=w[e].rearrange("(o p j) n -> p o (j n)", o=PASSES, j=PACK),
+                )
+                for oo in range(PASSES):
+                    raw[(e, oo)] = t[:, oo, :, :]
+            else:
+                t = keep.tile([P, PACK, N], F32, name=f"raw{e}_{o}")
+                nc.sync.dma_start(
+                    out=t[:].rearrange("p j n -> p (j n)"),
+                    in_=w[e, o * P * PACK : (o + 1) * P * PACK, :].rearrange("(p j) n -> p (j n)", j=PACK),
+                )
+                raw[(e, o)] = t[:]
+
+        def load_half(e, h, o):
+            whole = keep.tile([P, T if (e, h, o) in SUM_HOSTS else PACK * P], F32, name=f"raw{e}_{h}_{o}")
+            hosts[(e, h, o)] = whole
+            t = whole[:, : PACK * P].rearrange("p (j n) -> p j n", j=PACK)
+            nc.sync.dma_start(
+                out=t,
+                in_=w[e, o * P * PACK : (o + 1) * P * PACK, h * P : (h + 1) * P].rearrange("(p j) n -> p j n", j=PACK),
+            )
+            raw[(e, h, o)] = t
+
+        def load_gates(h):
+            for r in range(TOP):
+                nc.sync.dma_start(out=gates[h][r][:], in_=gate[r, h * P : (h + 1) * P, :])
+
+        nc.vector.memset(xs[:], 0)
+        for h in range(HALVES):
+            nc.vector.memset(y[h][:].rearrange("p (e c) -> p e c", c=C)[:, :, 0:1], 0.0)
+        nc.sync.dma_start(offs_sb[:], offs)
+        nc.sync.dma_start(
+            out=xw[:].rearrange("p (o t) -> p o t", o=PASSES),
+            in_=x_words.rearrange("o p t r -> p o (t r)").bitcast(I32),
+        )
+        load_whole(0, 0)
+        for q in range(4):
+            nc.sync.dma_start(
+                out=xs[32 * q : 32 * q + 4 * PASSES, :],
+                in_=x_scales[:, 4 * q : 4 * q + 4, :].bitcast(I32),
+            )
+        load_whole(0, 1)
+        load_whole(1, None)
+        nc.sync.dma_start(out=bias[:], in_=b.rearrange("(h p) e -> p h e", h=HALVES))
+        for e in range(2, WHOLE):
+            load_whole(e, None)
+            if e - 2 < TOP:
+                nc.sync.dma_start(pos_sb[e - 2][:], (pos1, pos2, pos3)[e - 2])
+        for h in range(HALVES):
+            for e in range(WHOLE, E):
+                for o in range(PASSES):
+                    load_half(e, h, o)
+            load_gates(h)
+
+        tok = {}
+
+        def gather_tokens(e):
+            for sort in range(PASSES + 1):
+                starts = STARTS[sort]
+                if e not in starts:
+                    continue
+                last = (starts + (E,))[starts.index(e) + 1]
+                n = (last - e) * C
+                idx = offs_sb[:, e * C // 16 : last * C // 16]
+                if sort < PASSES:
+                    t = ring_tok.tile([P, n], U32, name=f"tokw{sort}", align_bytes=64)
+                    nc.vector.tensor_copy(t[:], xw[:, sort * T : (sort + 1) * T].bitcast(U32).indirect(idx))
+                else:
+                    t = ring_tok.tile([P, n], U8, name="toks", align_bytes=64, bufs=3)
+                    nc.vector.tensor_copy(t[:], xs[:].bitcast(U8).indirect(idx))
+                for ee in range(e, last):
+                    tok[(sort, ee)] = (t, slice((ee - e) * C, (ee - e + 1) * C))
+
+        drains = [(e, h) for e in range(WHOLE) for h in range(HALVES)]
+        drains += [(e, h) for h in range(HALVES) for e in range(WHOLE, E)]
+        pins = {}
+        for e in range(2, WHOLE):
+            for o in range(PASSES):
+                pins[(e, None, o)] = (e - 2, o)
+        late = [(e, h) for e in (WHOLE - 2, WHOLE - 1) for h in range(HALVES)] + [(e, 0) for e in range(WHOLE, E - 1)]
+        spots = [(e, 0, o) for e in range(WHOLE, E) for o in range(PASSES)]
+        for i in range(4):
+            pins[spots[i]] = late[i]
+        for i in range(4, len(late)):
+            pins[spots[len(spots) - len(late) + i]] = late[i]
+        spots = [(e, 1, o) for e in range(WHOLE, E) for o in range(PASSES)]
+        late = [(e, 1) for e in range(WHOLE, E - 1)]
+        for i in range(len(late)):
+            pins[spots[len(spots) - len(late) + i]] = late[i]
+
+        def cast(dst, src, lo, hi, on_vector, key):
+            d = dst[:, lo:hi, :].rearrange("p (c i) j -> p c j i", i=4)
+            s = src[:, :, lo:hi].rearrange("p j (c i) -> p c j i", i=4)
+            if on_vector:
+                nc.vector.tensor_copy(out=d, in_=s)
+            elif key in pins:
+                pe, ph = pins[key]
+                nc.scalar.activation(out=d, in_=s, func=IDENT, bias=y[ph][:, pe * C : pe * C + 1])
+                pending.append((pe, ph))
+            else:
+                nc.scalar.activation(out=d, in_=s, func=IDENT)
+
+        def multiply(e, h, codes, scales, width, first, acc):
+            ts, ss = tok[(PASSES, e)]
+            for o in range(PASSES):
+                tw, ws = tok[(o, e)]
+                cols = slice(o * width + first, o * width + first + P)
+                nc.tensor.matmul_mx(
+                    out=acc,
+                    lhsT=codes[:, cols].bitcast(FP8X4),
+                    lhsT_scale=scales[:, cols],
+                    rhs=tw[:, ws].bitcast(FP8X4),
+                    rhs_scale=ts[4 * o : P, ss],
+                    start=(o == 0),
+                    stop=(o == PASSES - 1),
+                )
+            accs[(e, h)] = acc
+
+        def drain(e, h):
+            nc.scalar.activation(
+                out=y[h][:, e * C : (e + 1) * C], in_=accs[(e, h)], func=IDENT, bias=bias[:, h, e : e + 1]
+            )
+
+        accs = {}
+        pending = []
+
+        def flush():
+            for item in pending:
+                drain(*item)
+            pending.clear()
+
+        def expert_whole(e):
+            grouped = ring.tile([P, PASSES, N, PACK], BF16, name="grouped", align_bytes=64)
+            codes = ring.tile([P, PASSES * N], U32, name="codes", align_bytes=64)
+            scales = ring.tile([P, PASSES * N], U8, name="scales", align_bytes=64)
+            cast(grouped[:, 0], raw[(e, 0)], 0, N, False, (e, None, 0))
+            cast(grouped[:, 1], raw[(e, 1)], 0, N - 2 * VEC_WHOLE, False, (e, None, 1))
+            cast(grouped[:, 1], raw[(e, 1)], N - 2 * VEC_WHOLE, N, True, None)
+            flush()
+            nc.vector.quantize_mx(
+                out=codes[:].bitcast(FP8X4), scales=scales[:], in_=grouped[:].rearrange("p o n j -> p (o n j)")
+            )
+            acc = psum.tile([P, HALVES, C], F32, name="acc")
+            for h in range(HALVES):
+                multiply(e, h, codes, scales, N, h * P, acc[:, h, :])
+
+        def expert_half(e, h, vec_cols, by_pass):
+            grouped = ring_half.tile([P, PASSES, P, PACK], BF16, name="grouped_h", align_bytes=64)
+            codes = ring_half.tile([P, PASSES * P], U32, name="codes_h", align_bytes=64)
+            scales = ring_half.tile([P, PASSES * P], U8, name="scales_h", align_bytes=64)
+            for o in range(PASSES):
+                cut = P - vec_cols[o]
+                if cut > 0:
+                    cast(grouped[:, o], raw[(e, h, o)], 0, cut, False, (e, h, o))
+                if cut < P:
+                    cast(grouped[:, o], raw[(e, h, o)], cut, P, True, None)
+                if by_pass:
+                    nc.vector.quantize_mx(
+                        out=codes[:, o * P : (o + 1) * P].bitcast(FP8X4),
+                        scales=scales[:, o * P : (o + 1) * P],
+                        in_=grouped[:, o].rearrange("p n j -> p (n j)"),
+                    )
+            flush()
+            if not by_pass:
+                nc.vector.quantize_mx(
+                    out=codes[:].bitcast(FP8X4), scales=scales[:], in_=grouped[:].rearrange("p o n j -> p (o n j)")
+                )
+            acc = psum.tile([P, C], F32, name="acc")
+            multiply(e, h, codes, scales, P, 0, acc[:])
+            if e == E - 1:
+                drain(e, h)
+
+        prods = [[keep.tile([P, T], F32, name=f"prod{h}{r}") for r in range(TOP)] for h in range(HALVES)]
+
+        def fetch(h):
+            for r in range(TOP):
+                nc.vector.tensor_tensor(prods[h][r][:], y[h][:].indirect(pos_sb[r][:]), gates[h][r][:], MULT)
+
+        def add_up(h):
+            parts = (slice(0, FIRST_OUT), slice(FIRST_OUT, T))
+            for part in parts:
+                nc.vector.tensor_tensor(prods[h][0][:, part], prods[h][0][:, part], prods[h][1][:, part], ADD)
+            for part in parts:
+                nc.vector.tensor_tensor(prods[h][0][:, part], prods[h][0][:, part], prods[h][2][:, part], ADD)
+                nc.sync.dma_start(out=out[h * P : (h + 1) * P, part], in_=prods[h][0][:, part])
+
+        for e in range(E):
+            gather_tokens(e)
+            if e < WHOLE:
+                expert_whole(e)
+            else:
+                expert_half(e, 0, (0, 2 * VEC_HALF), e == E - 1)
+        flush()
+        fetch(0)
+        for e in range(WHOLE, E):
+            expert_half(e, 1, (0, 64 if e == E - 1 else 0), e == E - 1)
+        flush()
+        first = hosts[SUM_HOSTS[0]]
+        total = hosts[SUM_HOSTS[1]]
+        nc.vector.tensor_tensor(first[:], prods[0][0][:], prods[0][1][:], ADD)
+        nc.vector.tensor_tensor(total[:], first[:], prods[0][2][:], ADD)
+        nc.sync.dma_start(out=out[0:P, :], in_=total[:])
+        fetch(1)
+        add_up(1)

@@ -25,8 +25,8 @@ HALVES = N // P
 SPLIT = 5
 WHOLE = E - SPLIT
 GROUP = 3
-VEC_WHOLE = 64
-VEC_HALF = 32
+VEC_WHOLE = 96
+VEC_HALF = 48
 FIRST_OUT = 384
 SUM_HOSTS = ((E - 2, 1, 1), (E - 1, 1, 1))
 STARTS = ((0, 3, 6, 9, 12), (0, 1, 4, 7, 10, 13), (0, 2, 5, 8, 11, 14))
@@ -45,7 +45,7 @@ def tile_moe_pkd_lin_bias_kernel(
 
         offs_sb = keep.tile([P, S // 16], U16, name="offs_sb")
         pos_sb = [keep.tile([P, T // 16], U16, name=f"pos_sb{r}") for r in range(TOP)]
-        xw = keep.tile([P, PASSES * T], I32, name="xw", align_bytes=64)
+        xw = [keep.tile([P, T], I32, name=f"xw{o}", align_bytes=64) for o in range(PASSES)]
         xs = keep.tile([P, T // 4], I32, name="xs", align_bytes=64)
         bias = keep.tile([P, HALVES, E], F32, name="bias")
         gates = [[keep.tile([P, T], F32, name=f"gate{h}{r}") for r in range(TOP)] for h in range(HALVES)]
@@ -88,11 +88,9 @@ def tile_moe_pkd_lin_bias_kernel(
         for h in range(HALVES):
             nc.vector.memset(y[h][:].rearrange("p (e c) -> p e c", c=C)[:, :, 0:1], 0.0)
         nc.sync.dma_start(offs_sb[:], offs)
-        nc.sync.dma_start(
-            out=xw[:].rearrange("p (o t) -> p o t", o=PASSES),
-            in_=x_words.rearrange("o p t r -> p o (t r)").bitcast(I32),
-        )
+        nc.sync.dma_start(out=xw[0][:], in_=x_words[0].rearrange("p t r -> p (t r)").bitcast(I32))
         load_whole(0, 0)
+        nc.sync.dma_start(out=xw[1][:], in_=x_words[1].rearrange("p t r -> p (t r)").bitcast(I32))
         for q in range(4):
             nc.sync.dma_start(
                 out=xs[32 * q : 32 * q + 4 * PASSES, :],
@@ -123,29 +121,25 @@ def tile_moe_pkd_lin_bias_kernel(
                 idx = offs_sb[:, e * C // 16 : last * C // 16]
                 if sort < PASSES:
                     t = ring_tok.tile([P, n], U32, name=f"tokw{sort}", align_bytes=64)
-                    nc.vector.tensor_copy(t[:], xw[:, sort * T : (sort + 1) * T].bitcast(U32).indirect(idx))
+                    nc.vector.tensor_copy(t[:], xw[sort][:].bitcast(U32).indirect(idx))
                 else:
                     t = ring_tok.tile([P, n], U8, name="toks", align_bytes=64, bufs=3)
                     nc.vector.tensor_copy(t[:], xs[:].bitcast(U8).indirect(idx))
                 for ee in range(e, last):
                     tok[(sort, ee)] = (t, slice((ee - e) * C, (ee - e + 1) * C))
 
-        drains = [(e, h) for e in range(WHOLE) for h in range(HALVES)]
-        drains += [(e, h) for h in range(HALVES) for e in range(WHOLE, E)]
         pins = {}
-        for e in range(2, WHOLE):
+        for e in range(1, WHOLE):
             for o in range(PASSES):
-                pins[(e, None, o)] = (e - 2, o)
-        late = [(e, h) for e in (WHOLE - 2, WHOLE - 1) for h in range(HALVES)] + [(e, 0) for e in range(WHOLE, E - 1)]
-        spots = [(e, 0, o) for e in range(WHOLE, E) for o in range(PASSES)]
-        for i in range(4):
-            pins[spots[i]] = late[i]
-        for i in range(4, len(late)):
-            pins[spots[len(spots) - len(late) + i]] = late[i]
-        spots = [(e, 1, o) for e in range(WHOLE, E) for o in range(PASSES)]
-        late = [(e, 1) for e in range(WHOLE, E - 1)]
-        for i in range(len(late)):
-            pins[spots[len(spots) - len(late) + i]] = late[i]
+                pins[(e, None, o, 0)] = (e - 1, o)
+        pins[(WHOLE, 0, 0, 0)] = (WHOLE - 1, 0)
+        pins[(WHOLE, 0, 0, 1)] = (WHOLE - 1, 1)
+        for e in range(WHOLE + 2, E):
+            pins[(e, 0, 0, 0)] = (e - 2, 0)
+        spots = [(E - 2, 1, 1, 0), (E - 1, 1, 0, 0), (E - 1, 1, 0, 1), (E - 1, 1, 1, 0)]
+        for i in range(len(spots)):
+            pins[spots[i]] = (WHOLE + i, 1)
+        pinned = set(pins.values())
 
         def cast(dst, src, lo, hi, on_vector, key):
             d = dst[:, lo:hi, :].rearrange("p (c i) j -> p c j i", i=4)
@@ -192,9 +186,12 @@ def tile_moe_pkd_lin_bias_kernel(
             grouped = ring.tile([P, PASSES, N, PACK], BF16, name="grouped", align_bytes=64)
             codes = ring.tile([P, PASSES * N], U32, name="codes", align_bytes=64)
             scales = ring.tile([P, PASSES * N], U8, name="scales", align_bytes=64)
-            cast(grouped[:, 0], raw[(e, 0)], 0, N, False, (e, None, 0))
-            cast(grouped[:, 1], raw[(e, 1)], 0, N - 2 * VEC_WHOLE, False, (e, None, 1))
-            cast(grouped[:, 1], raw[(e, 1)], N - 2 * VEC_WHOLE, N, True, None)
+            cast(grouped[:, 0], raw[(e, 0)], 0, N, False, (e, None, 0, 0))
+            cast(grouped[:, 1], raw[(e, 1)], 0, N - 2 * VEC_WHOLE, False, (e, None, 1, 0))
+            lo = N - 2 * VEC_WHOLE
+            nc.gpsimd.tensor_scalar(
+                grouped[:, 1, lo:N, :], raw[(e, 1)][:, :, lo:N].rearrange("p j n -> p n j"), 1.0, 0.0, MULT, ADD
+            )
             flush()
             nc.vector.quantize_mx(
                 out=codes[:].bitcast(FP8X4), scales=scales[:], in_=grouped[:].rearrange("p o n j -> p (o n j)")
@@ -209,10 +206,22 @@ def tile_moe_pkd_lin_bias_kernel(
             scales = ring_half.tile([P, PASSES * P], U8, name="scales_h", align_bytes=64)
             for o in range(PASSES):
                 cut = P - vec_cols[o]
-                if cut > 0:
-                    cast(grouped[:, o], raw[(e, h, o)], 0, cut, False, (e, h, o))
-                if cut < P:
+                if (e, h, o, 1) in pins:
+                    cast(grouped[:, o], raw[(e, h, o)], 0, cut // 2, False, (e, h, o, 0))
+                    cast(grouped[:, o], raw[(e, h, o)], cut // 2, cut, False, (e, h, o, 1))
+                elif cut > 0:
+                    cast(grouped[:, o], raw[(e, h, o)], 0, cut, False, (e, h, o, 0))
+                if cut < P and (h == 1 or e == E - 1):
                     cast(grouped[:, o], raw[(e, h, o)], cut, P, True, None)
+                elif cut < P:
+                    nc.gpsimd.tensor_scalar(
+                        grouped[:, o, cut:P, :],
+                        raw[(e, h, o)][:, :, cut:P].rearrange("p j n -> p n j"),
+                        1.0,
+                        0.0,
+                        MULT,
+                        ADD,
+                    )
                 if by_pass:
                     nc.vector.quantize_mx(
                         out=codes[:, o * P : (o + 1) * P].bitcast(FP8X4),
@@ -228,6 +237,8 @@ def tile_moe_pkd_lin_bias_kernel(
             multiply(e, h, codes, scales, P, 0, acc[:])
             if e == E - 1:
                 drain(e, h)
+            elif (e, h) not in pinned:
+                pending.append((e, h))
 
         prods = [[keep.tile([P, T], F32, name=f"prod{h}{r}") for r in range(TOP)] for h in range(HALVES)]
 
@@ -248,7 +259,7 @@ def tile_moe_pkd_lin_bias_kernel(
             if e < WHOLE:
                 expert_whole(e)
             else:
-                expert_half(e, 0, (0, 2 * VEC_HALF), e == E - 1)
+                expert_half(e, 0, (0, 80 if e == E - 1 else 96), e == E - 1)
         flush()
         fetch(0)
         for e in range(WHOLE, E):

@@ -26,10 +26,8 @@ SPLIT = 5
 WHOLE = E - SPLIT
 GROUP = 3
 VEC_WHOLE = 96
-VEC_HALF = 48
 FIRST_OUT = 384
 SUM_HOSTS = ((E - 2, 1, 1), (E - 1, 1, 1))
-STARTS = ((0, 3, 6, 9, 12), (0, 1, 4, 7, 10, 13), (0, 2, 5, 8, 11, 14))
 
 
 def tile_moe_pkd_lin_bias_kernel(
@@ -40,7 +38,6 @@ def tile_moe_pkd_lin_bias_kernel(
         keep = ctx.enter_context(tc.tile_pool(name="keep", bufs=1))
         ring = ctx.enter_context(tc.tile_pool(name="ring", bufs=4))
         ring_half = ctx.enter_context(tc.tile_pool(name="ring_half", bufs=6))
-        ring_tok = ctx.enter_context(tc.tile_pool(name="ring_tok", bufs=2))
         psum = ctx.enter_context(tc.psum_pool(name="psum", bufs=8))
 
         offs_sb = keep.tile([P, S // 16], U16, name="offs_sb")
@@ -55,7 +52,7 @@ def tile_moe_pkd_lin_bias_kernel(
 
         def load_whole(e, o):
             if o is None:
-                t = keep.tile([P, PASSES, PACK, N], F32, name=f"raw{e}")
+                t = keep.tile([P, PASSES, PACK, N], F32, name=f"raw{e}", tag=f"slot{e}", align_bytes=64)
                 nc.sync.dma_start(
                     out=t[:].rearrange("p o j n -> p o (j n)"),
                     in_=w[e].rearrange("(o p j) n -> p o (j n)", o=PASSES, j=PACK),
@@ -63,7 +60,7 @@ def tile_moe_pkd_lin_bias_kernel(
                 for oo in range(PASSES):
                     raw[(e, oo)] = t[:, oo, :, :]
             else:
-                t = keep.tile([P, PACK, N], F32, name=f"raw{e}_{o}")
+                t = keep.tile([P, PACK, N], F32, name=f"raw{e}_{o}", tag=f"slot{e}" if o == 1 else f"first{e}", align_bytes=64)
                 nc.sync.dma_start(
                     out=t[:].rearrange("p j n -> p (j n)"),
                     in_=w[e, o * P * PACK : (o + 1) * P * PACK, :].rearrange("(p j) n -> p (j n)", j=PACK),
@@ -111,22 +108,18 @@ def tile_moe_pkd_lin_bias_kernel(
 
         tok = {}
 
-        def gather_tokens(e):
-            for sort in range(PASSES + 1):
-                starts = STARTS[sort]
-                if e not in starts:
-                    continue
-                last = (starts + (E,))[starts.index(e) + 1]
-                n = (last - e) * C
-                idx = offs_sb[:, e * C // 16 : last * C // 16]
-                if sort < PASSES:
-                    t = ring_tok.tile([P, n], U32, name=f"tokw{sort}", align_bytes=64)
-                    nc.vector.tensor_copy(t[:], xw[sort][:].bitcast(U32).indirect(idx))
-                else:
-                    t = ring_tok.tile([P, n], U8, name="toks", align_bytes=64, bufs=3)
-                    nc.vector.tensor_copy(t[:], xs[:].bitcast(U8).indirect(idx))
-                for ee in range(e, last):
-                    tok[(sort, ee)] = (t, slice((ee - e) * C, (ee - e + 1) * C))
+        def gather_tokens(index, tag):
+            g, sort = divmod(index, PASSES + 1)
+            n = GROUP * C
+            idx = offs_sb[:, g * n // 16 : (g + 1) * n // 16]
+            if sort < PASSES:
+                t = keep.tile([P, n], U32, name=f"tok{index}", tag=tag, align_bytes=64)
+                nc.vector.tensor_copy(t[:], xw[sort][:].bitcast(U32).indirect(idx))
+            else:
+                t = keep.tile([P, n], U8, name=f"tok{index}", tag=tag, align_bytes=64)
+                nc.vector.tensor_copy(t[:], xs[:].bitcast(U8).indirect(idx))
+            for i in range(GROUP):
+                tok[(sort, g * GROUP + i)] = (t, slice(i * C, (i + 1) * C))
 
         pins = {}
         for e in range(1, WHOLE):
@@ -254,10 +247,13 @@ def tile_moe_pkd_lin_bias_kernel(
                 nc.vector.tensor_tensor(prods[h][0][:, part], prods[h][0][:, part], prods[h][2][:, part], ADD)
                 nc.sync.dma_start(out=out[h * P : (h + 1) * P, part], in_=prods[h][0][:, part])
 
+        early = (PASSES + 1) * (E // GROUP) - WHOLE
+        for index in range(early):
+            gather_tokens(index, f"tok{index}")
         for e in range(E):
-            gather_tokens(e)
             if e < WHOLE:
                 expert_whole(e)
+                gather_tokens(early + e, f"slot{e}")
             else:
                 expert_half(e, 0, (0, 80 if e == E - 1 else 96), e == E - 1)
         flush()

@@ -25,7 +25,7 @@ HALVES = N // P
 SPLIT = 5
 WHOLE = E - SPLIT
 GROUP = 3
-VEC_WHOLE = 96
+VEC_WHOLE = 64
 FIRST_OUT = 384
 SUM_HOSTS = ((E - 2, 1, 1), (E - 1, 1, 1))
 
@@ -122,11 +122,9 @@ def tile_moe_pkd_lin_bias_kernel(
                 tok[(sort, g * GROUP + i)] = (t, slice(i * C, (i + 1) * C))
 
         pins = {}
-        for e in range(1, WHOLE):
+        for e in range(2, WHOLE + 2):
             for o in range(PASSES):
-                pins[(e, None, o, 0)] = (e - 1, o)
-        pins[(WHOLE, 0, 0, 0)] = (WHOLE - 1, 0)
-        pins[(WHOLE, 0, 0, 1)] = (WHOLE - 1, 1)
+                pins[(e, None if e < WHOLE else 0, o, 0)] = (e - 2, o)
         for e in range(WHOLE + 2, E):
             pins[(e, 0, 0, 0)] = (e - 2, 0)
         spots = [(E - 2, 1, 1, 0), (E - 1, 1, 0, 0), (E - 1, 1, 0, 1), (E - 1, 1, 1, 0)]
@@ -175,17 +173,17 @@ def tile_moe_pkd_lin_bias_kernel(
                 drain(*item)
             pending.clear()
 
+        early = (PASSES + 1) * (E // GROUP) - WHOLE
+
         def expert_whole(e):
             grouped = ring.tile([P, PASSES, N, PACK], BF16, name="grouped", align_bytes=64)
             codes = ring.tile([P, PASSES * N], U32, name="codes", align_bytes=64)
             scales = ring.tile([P, PASSES * N], U8, name="scales", align_bytes=64)
             cast(grouped[:, 0], raw[(e, 0)], 0, N, False, (e, None, 0, 0))
             cast(grouped[:, 1], raw[(e, 1)], 0, N - 2 * VEC_WHOLE, False, (e, None, 1, 0))
-            lo = N - 2 * VEC_WHOLE
-            nc.gpsimd.tensor_scalar(
-                grouped[:, 1, lo:N, :], raw[(e, 1)][:, :, lo:N].rearrange("p j n -> p n j"), 1.0, 0.0, MULT, ADD
-            )
+            cast(grouped[:, 1], raw[(e, 1)], N - 2 * VEC_WHOLE, N, True, None)
             flush()
+            gather_tokens(early + e, f"slot{e}")
             nc.vector.quantize_mx(
                 out=codes[:].bitcast(FP8X4), scales=scales[:], in_=grouped[:].rearrange("p o n j -> p (o n j)")
             )
@@ -204,17 +202,8 @@ def tile_moe_pkd_lin_bias_kernel(
                     cast(grouped[:, o], raw[(e, h, o)], cut // 2, cut, False, (e, h, o, 1))
                 elif cut > 0:
                     cast(grouped[:, o], raw[(e, h, o)], 0, cut, False, (e, h, o, 0))
-                if cut < P and (h == 1 or e == E - 1):
+                if cut < P:
                     cast(grouped[:, o], raw[(e, h, o)], cut, P, True, None)
-                elif cut < P:
-                    nc.gpsimd.tensor_scalar(
-                        grouped[:, o, cut:P, :],
-                        raw[(e, h, o)][:, :, cut:P].rearrange("p j n -> p n j"),
-                        1.0,
-                        0.0,
-                        MULT,
-                        ADD,
-                    )
                 if by_pass:
                     nc.vector.quantize_mx(
                         out=codes[:, o * P : (o + 1) * P].bitcast(FP8X4),
@@ -247,15 +236,13 @@ def tile_moe_pkd_lin_bias_kernel(
                 nc.vector.tensor_tensor(prods[h][0][:, part], prods[h][0][:, part], prods[h][2][:, part], ADD)
                 nc.sync.dma_start(out=out[h * P : (h + 1) * P, part], in_=prods[h][0][:, part])
 
-        early = (PASSES + 1) * (E // GROUP) - WHOLE
         for index in range(early):
             gather_tokens(index, f"tok{index}")
         for e in range(E):
             if e < WHOLE:
                 expert_whole(e)
-                gather_tokens(early + e, f"slot{e}")
             else:
-                expert_half(e, 0, (0, 80 if e == E - 1 else 96), e == E - 1)
+                expert_half(e, 0, (0, 80 if e == E - 1 else 64), e == E - 1)
         flush()
         fetch(0)
         for e in range(WHOLE, E):

@@ -1,6 +1,7 @@
 from contextlib import ExitStack
 
 import concourse.mybir as mybir
+from concourse.masks import make_identity
 
 K, T, E, C, N = 1024, 640, 15, 128, 256
 TOP = 3
@@ -22,12 +23,24 @@ P = 128
 PACK = 4
 PASSES = K // (P * PACK)
 HALVES = N // P
-SPLIT = 5
-WHOLE = E - SPLIT
+QUADRANTS = 4
+ROWS = 4
+PER_COLUMN = 16
+LAST = E - 1
+BY_PASS = (0, E - 2, E - 1)
+LAG = 2
+RUN = 4
+
 GROUP = 3
-VEC_WHOLE = 64
-FIRST_OUT = 384
-SUM_HOSTS = ((E - 2, 1, 1), (E - 1, 1, 1))
+SORTS = PASSES + 1
+GATHERS = SORTS * (E // GROUP)
+GATHERING = 10
+
+VECTOR_COLUMNS_GATHERING = 144
+VECTOR_COLUMNS_LATER = 240
+VECTOR_COLUMNS_LAST = 80
+
+FIRST_PIECE = 384
 
 
 def tile_moe_pkd_lin_bias_kernel(
@@ -37,221 +50,205 @@ def tile_moe_pkd_lin_bias_kernel(
     with ExitStack() as ctx:
         keep = ctx.enter_context(tc.tile_pool(name="keep", bufs=1))
         ring = ctx.enter_context(tc.tile_pool(name="ring", bufs=4))
-        ring_half = ctx.enter_context(tc.tile_pool(name="ring_half", bufs=6))
+        ring_half = ctx.enter_context(tc.tile_pool(name="ring_half", bufs=HALVES))
         psum = ctx.enter_context(tc.psum_pool(name="psum", bufs=8))
 
-        offs_sb = keep.tile([P, S // 16], U16, name="offs_sb")
-        pos_sb = [keep.tile([P, T // 16], U16, name=f"pos_sb{r}") for r in range(TOP)]
+        offs_sb = keep.tile([P, S // PER_COLUMN], U16, name="offs_sb")
+        pos_sb = [keep.tile([P, T // PER_COLUMN], U16, name=f"pos_sb{r}") for r in range(TOP)]
         xw = [keep.tile([P, T], I32, name=f"xw{o}", align_bytes=64) for o in range(PASSES)]
         xs = keep.tile([P, T // 4], I32, name="xs", align_bytes=64)
         bias = keep.tile([P, HALVES, E], F32, name="bias")
         gates = [[keep.tile([P, T], F32, name=f"gate{h}{r}") for r in range(TOP)] for h in range(HALVES)]
         y = [keep.tile([P, S], F32, name=f"y{h}") for h in range(HALVES)]
         raw = {}
-        hosts = {}
 
-        def load_whole(e, o):
-            if o is None:
-                t = keep.tile([P, PASSES, PACK, N], F32, name=f"raw{e}", tag=f"slot{e}", align_bytes=64)
-                nc.sync.dma_start(
-                    out=t[:].rearrange("p o j n -> p o (j n)"),
-                    in_=w[e].rearrange("(o p j) n -> p o (j n)", o=PASSES, j=PACK),
-                )
-                for oo in range(PASSES):
-                    raw[(e, oo)] = t[:, oo, :, :]
-            else:
-                t = keep.tile([P, PACK, N], F32, name=f"raw{e}_{o}", tag=f"slot{e}" if o == 1 else f"first{e}", align_bytes=64)
-                nc.sync.dma_start(
-                    out=t[:].rearrange("p j n -> p (j n)"),
-                    in_=w[e, o * P * PACK : (o + 1) * P * PACK, :].rearrange("(p j) n -> p (j n)", j=PACK),
-                )
-                raw[(e, o)] = t[:]
-
-        def load_half(e, h, o):
-            whole = keep.tile([P, T if (e, h, o) in SUM_HOSTS else PACK * P], F32, name=f"raw{e}_{h}_{o}")
-            hosts[(e, h, o)] = whole
-            t = whole[:, : PACK * P].rearrange("p (j n) -> p j n", j=PACK)
+        def load_expert(e):
+            both = keep.tile([P, PASSES, PACK, N], F32, name=f"raw{e}", tag=f"place{e}", align_bytes=64)
             nc.sync.dma_start(
-                out=t,
-                in_=w[e, o * P * PACK : (o + 1) * P * PACK, h * P : (h + 1) * P].rearrange("(p j) n -> p j n", j=PACK),
+                out=both[:].rearrange("p o j n -> p o (j n)"),
+                in_=w[e].rearrange("(o p j) n -> p o (j n)", o=PASSES, j=PACK),
             )
-            raw[(e, h, o)] = t
+            for o in range(PASSES):
+                raw[(e, o)] = both[:, o, :, :]
 
-        def load_gates(h):
-            for r in range(TOP):
-                nc.sync.dma_start(out=gates[h][r][:], in_=gate[r, h * P : (h + 1) * P, :])
+        def load_pass(e, o):
+            tag = f"place{e}" if o == PASSES - 1 else f"early{e}"
+            one = keep.tile([P, PACK, N], F32, name=f"raw{e}_{o}", tag=tag, align_bytes=64)
+            nc.sync.dma_start(
+                out=one[:].rearrange("p j n -> p (j n)"),
+                in_=w[e, o * P * PACK : (o + 1) * P * PACK, :].rearrange("(p j) n -> p (j n)", j=PACK),
+            )
+            raw[(e, o)] = one[:]
 
         nc.vector.memset(xs[:], 0)
         for h in range(HALVES):
-            nc.vector.memset(y[h][:].rearrange("p (e c) -> p e c", c=C)[:, :, 0:1], 0.0)
+            nc.vector.memset(y[h][:].rearrange("p (e c) -> p e c", c=C)[:, :LAST, 0:1], 0.0)
+
         nc.sync.dma_start(offs_sb[:], offs)
         nc.sync.dma_start(out=xw[0][:], in_=x_words[0].rearrange("p t r -> p (t r)").bitcast(I32))
-        load_whole(0, 0)
+        load_pass(0, 0)
         nc.sync.dma_start(out=xw[1][:], in_=x_words[1].rearrange("p t r -> p (t r)").bitcast(I32))
-        for q in range(4):
+        for q in range(QUADRANTS):
             nc.sync.dma_start(
-                out=xs[32 * q : 32 * q + 4 * PASSES, :],
-                in_=x_scales[:, 4 * q : 4 * q + 4, :].bitcast(I32),
+                out=xs[32 * q : 32 * q + ROWS * PASSES, :],
+                in_=x_scales[:, ROWS * q : ROWS * (q + 1), :].bitcast(I32),
             )
-        load_whole(0, 1)
-        load_whole(1, None)
+        load_pass(0, 1)
+        load_expert(1)
         nc.sync.dma_start(out=bias[:], in_=b.rearrange("(h p) e -> p h e", h=HALVES))
-        for e in range(2, WHOLE):
-            load_whole(e, None)
-            if e - 2 < TOP:
-                nc.sync.dma_start(pos_sb[e - 2][:], (pos1, pos2, pos3)[e - 2])
-        for h in range(HALVES):
-            for e in range(WHOLE, E):
+        small = list(zip(pos_sb, (pos1, pos2, pos3)))
+        for e in range(2, E):
+            if e in BY_PASS:
                 for o in range(PASSES):
-                    load_half(e, h, o)
-            load_gates(h)
+                    load_pass(e, o)
+            else:
+                load_expert(e)
+            for list_sb, list_hbm in small[e - 2 : e - 1]:
+                nc.sync.dma_start(list_sb[:], list_hbm)
+        for h in range(HALVES):
+            for r in range(TOP):
+                nc.sync.dma_start(out=gates[h][r][:], in_=gate[r, h * P : (h + 1) * P, :])
+        ident = keep.tile([P, P], F32, name="ident")
+        make_identity(nc, ident[:])
 
-        tok = {}
+        tokens = {}
+        sums = {}
 
         def gather_tokens(index, tag):
-            g, sort = divmod(index, PASSES + 1)
-            n = GROUP * C
-            idx = offs_sb[:, g * n // 16 : (g + 1) * n // 16]
-            if sort < PASSES:
-                t = keep.tile([P, n], U32, name=f"tok{index}", tag=tag, align_bytes=64)
-                nc.vector.tensor_copy(t[:], xw[sort][:].bitcast(U32).indirect(idx))
-            else:
-                t = keep.tile([P, n], U8, name=f"tok{index}", tag=tag, align_bytes=64)
-                nc.vector.tensor_copy(t[:], xs[:].bitcast(U8).indirect(idx))
+            group, sort = divmod(index, SORTS)
+            count = GROUP * C
+            entries = offs_sb[:, group * count // PER_COLUMN : (group + 1) * count // PER_COLUMN]
+            window = xw[sort][:].bitcast(U32) if sort < PASSES else xs[:].bitcast(U8)
+            picked = keep.tile(
+                [P, count], U32 if sort < PASSES else U8, name=f"picked{index}", tag=tag, align_bytes=64
+            )
+            nc.vector.tensor_copy(picked[:], window.indirect(entries))
             for i in range(GROUP):
-                tok[(sort, g * GROUP + i)] = (t, slice(i * C, (i + 1) * C))
+                tokens[(sort, group * GROUP + i)] = (picked, slice(i * C, (i + 1) * C))
 
-        pins = {}
-        for e in range(2, WHOLE + 2):
-            for o in range(PASSES):
-                pins[(e, None if e < WHOLE else 0, o, 0)] = (e - 2, o)
-        for e in range(WHOLE + 2, E):
-            pins[(e, 0, 0, 0)] = (e - 2, 0)
-        spots = [(E - 2, 1, 1, 0), (E - 1, 1, 0, 0), (E - 1, 1, 0, 1), (E - 1, 1, 1, 0)]
-        for i in range(len(spots)):
-            pins[spots[i]] = (WHOLE + i, 1)
-        pinned = set(pins.values())
+        def interleaved(dst, src, lo, hi):
+            return (
+                dst[:, lo:hi, :].rearrange("p (c i) j -> p c j i", i=RUN),
+                src[:, :, lo:hi].rearrange("p j (c i) -> p c j i", i=RUN),
+            )
 
-        def cast(dst, src, lo, hi, on_vector, key):
-            d = dst[:, lo:hi, :].rearrange("p (c i) j -> p c j i", i=4)
-            s = src[:, :, lo:hi].rearrange("p j (c i) -> p c j i", i=4)
-            if on_vector:
-                nc.vector.tensor_copy(out=d, in_=s)
-            elif key in pins:
-                pe, ph = pins[key]
-                nc.scalar.activation(out=d, in_=s, func=IDENT, bias=y[ph][:, pe * C : pe * C + 1])
-                pending.append((pe, ph))
+        def round_on_vector(dst, src, lo, hi):
+            to, source = interleaved(dst, src, lo, hi)
+            nc.vector.tensor_copy(out=to, in_=source)
+
+        def round_on_scalar(dst, src, lo, hi, e, h):
+            to, source = interleaved(dst, src, lo, hi)
+            if e < 0:
+                nc.scalar.activation(out=to, in_=source, func=IDENT)
             else:
-                nc.scalar.activation(out=d, in_=s, func=IDENT)
+                nc.scalar.activation(out=to, in_=source, func=IDENT, bias=y[h][:, e * C : e * C + 1])
+
+        def quantize(codes, scales, rounded):
+            nc.vector.quantize_mx(out=codes.bitcast(FP8X4), scales=scales, in_=rounded)
 
         def multiply(e, h, codes, scales, width, first, acc):
-            ts, ss = tok[(PASSES, e)]
+            token_scales, scale_slots = tokens[(PASSES, e)]
             for o in range(PASSES):
-                tw, ws = tok[(o, e)]
+                token_words, word_slots = tokens[(o, e)]
                 cols = slice(o * width + first, o * width + first + P)
                 nc.tensor.matmul_mx(
                     out=acc,
                     lhsT=codes[:, cols].bitcast(FP8X4),
                     lhsT_scale=scales[:, cols],
-                    rhs=tw[:, ws].bitcast(FP8X4),
-                    rhs_scale=ts[4 * o : P, ss],
+                    rhs=token_words[:, word_slots].bitcast(FP8X4),
+                    rhs_scale=token_scales[ROWS * o : P, scale_slots],
                     start=(o == 0),
                     stop=(o == PASSES - 1),
                 )
-            accs[(e, h)] = acc
+            sums[(e, h)] = acc
 
         def drain(e, h):
             nc.scalar.activation(
-                out=y[h][:, e * C : (e + 1) * C], in_=accs[(e, h)], func=IDENT, bias=bias[:, h, e : e + 1]
+                out=y[h][:, e * C : (e + 1) * C], in_=sums[(e, h)], func=IDENT, bias=bias[:, h, e : e + 1]
             )
 
-        accs = {}
-        pending = []
-
-        def flush():
-            for item in pending:
-                drain(*item)
-            pending.clear()
-
-        early = (PASSES + 1) * (E // GROUP) - WHOLE
-
-        def expert_whole(e):
-            grouped = ring.tile([P, PASSES, N, PACK], BF16, name="grouped", align_bytes=64)
+        def whole_expert(e):
+            rounded = ring.tile([P, PASSES, N, PACK], BF16, name="rounded", align_bytes=64)
             codes = ring.tile([P, PASSES * N], U32, name="codes", align_bytes=64)
             scales = ring.tile([P, PASSES * N], U8, name="scales", align_bytes=64)
-            cast(grouped[:, 0], raw[(e, 0)], 0, N, False, (e, None, 0, 0))
-            cast(grouped[:, 1], raw[(e, 1)], 0, N - 2 * VEC_WHOLE, False, (e, None, 1, 0))
-            cast(grouped[:, 1], raw[(e, 1)], N - 2 * VEC_WHOLE, N, True, None)
-            flush()
-            gather_tokens(early + e, f"slot{e}")
-            nc.vector.quantize_mx(
-                out=codes[:].bitcast(FP8X4), scales=scales[:], in_=grouped[:].rearrange("p o n j -> p (o n j)")
-            )
-            acc = psum.tile([P, HALVES, C], F32, name="acc")
+            cut = N - (VECTOR_COLUMNS_GATHERING if e < GATHERING else VECTOR_COLUMNS_LATER)
+            round_on_scalar(rounded[:, 0], raw[(e, 0)], 0, N, e - LAG, 0)
+            round_on_scalar(rounded[:, 1], raw[(e, 1)], 0, cut, e - LAG, 1)
+            round_on_vector(rounded[:, 1], raw[(e, 1)], cut, N)
+            if e >= LAG:
+                for h in range(HALVES):
+                    drain(e - LAG, h)
+            if e < GATHERING:
+                gather_tokens(GATHERS - GATHERING + e, f"place{e}")
+            quantize(codes[:], scales[:], rounded[:].rearrange("p o n j -> p (o n j)"))
+            acc = psum.tile([P, HALVES, C], F32, name="acc", tag="bank")
             for h in range(HALVES):
                 multiply(e, h, codes, scales, N, h * P, acc[:, h, :])
 
-        def expert_half(e, h, vec_cols, by_pass):
-            grouped = ring_half.tile([P, PASSES, P, PACK], BF16, name="grouped_h", align_bytes=64)
-            codes = ring_half.tile([P, PASSES * P], U32, name="codes_h", align_bytes=64)
-            scales = ring_half.tile([P, PASSES * P], U8, name="scales_h", align_bytes=64)
+        def last_expert_half(h):
+            rounded = ring_half.tile([P, PASSES, P, PACK], BF16, name="rounded_half", align_bytes=64)
+            codes = ring_half.tile([P, PASSES * P], U32, name="codes_half", align_bytes=64)
+            scales = ring_half.tile([P, PASSES * P], U8, name="scales_half", align_bytes=64)
             for o in range(PASSES):
-                cut = P - vec_cols[o]
-                if (e, h, o, 1) in pins:
-                    cast(grouped[:, o], raw[(e, h, o)], 0, cut // 2, False, (e, h, o, 0))
-                    cast(grouped[:, o], raw[(e, h, o)], cut // 2, cut, False, (e, h, o, 1))
-                elif cut > 0:
-                    cast(grouped[:, o], raw[(e, h, o)], 0, cut, False, (e, h, o, 0))
-                if cut < P:
-                    cast(grouped[:, o], raw[(e, h, o)], cut, P, True, None)
-                if by_pass:
-                    nc.vector.quantize_mx(
-                        out=codes[:, o * P : (o + 1) * P].bitcast(FP8X4),
-                        scales=scales[:, o * P : (o + 1) * P],
-                        in_=grouped[:, o].rearrange("p n j -> p (n j)"),
-                    )
-            flush()
-            if not by_pass:
-                nc.vector.quantize_mx(
-                    out=codes[:].bitcast(FP8X4), scales=scales[:], in_=grouped[:].rearrange("p o n j -> p (o n j)")
-                )
-            acc = psum.tile([P, C], F32, name="acc")
-            multiply(e, h, codes, scales, P, 0, acc[:])
-            if e == E - 1:
-                drain(e, h)
-            elif (e, h) not in pinned:
-                pending.append((e, h))
+                source = raw[(LAST, o)][:, :, h * P : (h + 1) * P]
+                shared = h == 0 and o == PASSES - 1
+                cut = P - VECTOR_COLUMNS_LAST if shared else P
+                round_on_scalar(rounded[:, o], source, 0, cut, LAST - LAG + o, h)
+                if shared:
+                    round_on_vector(rounded[:, o], source, cut, P)
+                if h == 0:
+                    cols = slice(o * P, (o + 1) * P)
+                    quantize(codes[:, cols], scales[:, cols], rounded[:, o].rearrange("p n j -> p (n j)"))
+            for o in range(PASSES):
+                drain(LAST - LAG + o, h)
+            if h > 0:
+                quantize(codes[:], scales[:], rounded[:].rearrange("p o n j -> p (o n j)"))
+            acc = psum.tile([P, C], F32, name="acc_half", tag="bank")
+            multiply(LAST, h, codes, scales, P, 0, acc[:])
+            drain(LAST, h)
 
-        prods = [[keep.tile([P, T], F32, name=f"prod{h}{r}") for r in range(TOP)] for h in range(HALVES)]
+        products = [[keep.tile([P, T], F32, name=f"product{h}{r}") for r in range(TOP)] for h in range(HALVES)]
 
-        def fetch(h):
+        for index in range(GATHERS - GATHERING):
+            gather_tokens(index, f"picked{index}")
+        for e in range(LAST):
+            whole_expert(e)
+        for h in range(HALVES):
+            last_expert_half(h)
+        for h in range(HALVES):
             for r in range(TOP):
-                nc.vector.tensor_tensor(prods[h][r][:], y[h][:].indirect(pos_sb[r][:]), gates[h][r][:], MULT)
+                nc.vector.tensor_tensor(products[h][r][:], y[h][:].indirect(pos_sb[r][:]), gates[h][r][:], MULT)
 
-        def add_up(h):
-            parts = (slice(0, FIRST_OUT), slice(FIRST_OUT, T))
-            for part in parts:
-                nc.vector.tensor_tensor(prods[h][0][:, part], prods[h][0][:, part], prods[h][1][:, part], ADD)
-            for part in parts:
-                nc.vector.tensor_tensor(prods[h][0][:, part], prods[h][0][:, part], prods[h][2][:, part], ADD)
-                nc.sync.dma_start(out=out[h * P : (h + 1) * P, part], in_=prods[h][0][:, part])
+        pieces = (slice(0, FIRST_PIECE), slice(FIRST_PIECE, T))
+        blocks = [slice(i * P, (i + 1) * P) for i in range(T // P)]
 
-        for index in range(early):
-            gather_tokens(index, f"tok{index}")
-        for e in range(E):
-            if e < WHOLE:
-                expert_whole(e)
-            else:
-                expert_half(e, 0, (0, 80 if e == E - 1 else 64), e == E - 1)
-        flush()
-        fetch(0)
-        for e in range(WHOLE, E):
-            expert_half(e, 1, (0, 64 if e == E - 1 else 0), e == E - 1)
-        flush()
-        first = hosts[SUM_HOSTS[0]]
-        total = hosts[SUM_HOSTS[1]]
-        nc.vector.tensor_tensor(first[:], prods[0][0][:], prods[0][1][:], ADD)
-        nc.vector.tensor_tensor(total[:], first[:], prods[0][2][:], ADD)
+        total = keep.tile([P, T], F32, name="total")
+        turned = [psum.tile([P, P], F32, name=f"turned{i}", tag="bank") for i in range(len(blocks))]
+        for r in range(TOP):
+            for bank, block in zip(turned, blocks):
+                nc.tensor.matmul(
+                    bank[:],
+                    products[0][r][:, block],
+                    ident[:],
+                    start=(r == 0),
+                    stop=(r == TOP - 1),
+                    is_transpose=True,
+                )
+        staged = keep.tile([P, T], F32, name="staged")
+        for bank, block in zip(turned, blocks):
+            nc.scalar.copy(staged[:, block], bank[:])
+        for piece in pieces:
+            back = psum.tile([P, piece.stop - piece.start], F32, name="back", tag="bank")
+            for block in blocks[piece.start // P : piece.stop // P]:
+                nc.tensor.transpose(
+                    back[:, block.start - piece.start : block.stop - piece.start], staged[:, block], ident[:]
+                )
+            nc.scalar.copy(total[:, piece], back[:])
         nc.sync.dma_start(out=out[0:P, :], in_=total[:])
-        fetch(1)
-        add_up(1)
+
+        running = products[1][0]
+        for r in range(1, TOP):
+            for piece in pieces:
+                nc.vector.tensor_tensor(running[:, piece], running[:, piece], products[1][r][:, piece], ADD)
+                if r == TOP - 1:
+                    nc.sync.dma_start(out=out[P:N, piece], in_=running[:, piece])

from contextlib import ExitStack

import concourse.mybir as mybir
from concourse.masks import make_identity

K, T, E, C, N = 1024, 640, 15, 128, 256
TOP = 3
S = E * C
FLOPS = 2 * K * N * S

F32 = mybir.dt.float32
BF16 = mybir.dt.bfloat16
I32 = mybir.dt.int32
U32 = mybir.dt.uint32
U16 = mybir.dt.uint16
U8 = mybir.dt.uint8
FP8X4 = mybir.dt.float8_e4m3fn_x4
IDENT = mybir.ActivationFunctionType.Identity
MULT = mybir.AluOpType.mult
ADD = mybir.AluOpType.add

P = 128
PACK = 4
PASSES = K // (P * PACK)
HALVES = N // P
QUADRANTS = 4
ROWS = 4
PER_COLUMN = 16
LAST = E - 1
BY_PASS = (0, E - 2, E - 1)
LAG = 2
RUN = 4

GROUP = 3
SORTS = PASSES + 1
GATHERS = SORTS * (E // GROUP)
GATHERING = 10

VECTOR_COLUMNS_GATHERING = 144
VECTOR_COLUMNS_LATER = 240
VECTOR_COLUMNS_LAST = 80

FIRST_PIECE = 384


def tile_moe_pkd_lin_bias_kernel(
    tc, x_words, x_scales, w, b, gate, offs, pos1, pos2, pos3, out
):
    nc = tc.nc
    with ExitStack() as ctx:
        keep = ctx.enter_context(tc.tile_pool(name="keep", bufs=1))
        ring = ctx.enter_context(tc.tile_pool(name="ring", bufs=4))
        ring_half = ctx.enter_context(tc.tile_pool(name="ring_half", bufs=HALVES))
        psum = ctx.enter_context(tc.psum_pool(name="psum", bufs=8))

        offs_sb = keep.tile([P, S // PER_COLUMN], U16, name="offs_sb")
        pos_sb = [keep.tile([P, T // PER_COLUMN], U16, name=f"pos_sb{r}") for r in range(TOP)]
        xw = [keep.tile([P, T], I32, name=f"xw{o}", align_bytes=64) for o in range(PASSES)]
        xs = keep.tile([P, T // 4], I32, name="xs", align_bytes=64)
        bias = keep.tile([P, HALVES, E], F32, name="bias")
        gates = [[keep.tile([P, T], F32, name=f"gate{h}{r}") for r in range(TOP)] for h in range(HALVES)]
        y = [keep.tile([P, S], F32, name=f"y{h}") for h in range(HALVES)]
        raw = {}

        def load_expert(e):
            both = keep.tile([P, PASSES, PACK, N], F32, name=f"raw{e}", tag=f"place{e}", align_bytes=64)
            nc.sync.dma_start(
                out=both[:].rearrange("p o j n -> p o (j n)"),
                in_=w[e].rearrange("(o p j) n -> p o (j n)", o=PASSES, j=PACK),
            )
            for o in range(PASSES):
                raw[(e, o)] = both[:, o, :, :]

        def load_pass(e, o):
            tag = f"place{e}" if o == PASSES - 1 else f"early{e}"
            one = keep.tile([P, PACK, N], F32, name=f"raw{e}_{o}", tag=tag, align_bytes=64)
            nc.sync.dma_start(
                out=one[:].rearrange("p j n -> p (j n)"),
                in_=w[e, o * P * PACK : (o + 1) * P * PACK, :].rearrange("(p j) n -> p (j n)", j=PACK),
            )
            raw[(e, o)] = one[:]

        nc.vector.memset(xs[:], 0)
        for h in range(HALVES):
            nc.vector.memset(y[h][:].rearrange("p (e c) -> p e c", c=C)[:, :LAST, 0:1], 0.0)

        nc.sync.dma_start(offs_sb[:], offs)
        nc.sync.dma_start(out=xw[0][:], in_=x_words[0].rearrange("p t r -> p (t r)").bitcast(I32))
        load_pass(0, 0)
        nc.sync.dma_start(out=xw[1][:], in_=x_words[1].rearrange("p t r -> p (t r)").bitcast(I32))
        for q in range(QUADRANTS):
            nc.sync.dma_start(
                out=xs[32 * q : 32 * q + ROWS * PASSES, :],
                in_=x_scales[:, ROWS * q : ROWS * (q + 1), :].bitcast(I32),
            )
        load_pass(0, 1)
        load_expert(1)
        nc.sync.dma_start(out=bias[:], in_=b.rearrange("(h p) e -> p h e", h=HALVES))
        small = list(zip(pos_sb, (pos1, pos2, pos3)))
        for e in range(2, E):
            if e in BY_PASS:
                for o in range(PASSES):
                    load_pass(e, o)
            else:
                load_expert(e)
            for list_sb, list_hbm in small[e - 2 : e - 1]:
                nc.sync.dma_start(list_sb[:], list_hbm)
        for h in range(HALVES):
            for r in range(TOP):
                nc.sync.dma_start(out=gates[h][r][:], in_=gate[r, h * P : (h + 1) * P, :])
        ident = keep.tile([P, P], F32, name="ident")
        make_identity(nc, ident[:])

        tokens = {}
        sums = {}

        def gather_tokens(index, tag):
            group, sort = divmod(index, SORTS)
            count = GROUP * C
            entries = offs_sb[:, group * count // PER_COLUMN : (group + 1) * count // PER_COLUMN]
            window = xw[sort][:].bitcast(U32) if sort < PASSES else xs[:].bitcast(U8)
            picked = keep.tile(
                [P, count], U32 if sort < PASSES else U8, name=f"picked{index}", tag=tag, align_bytes=64
            )
            nc.vector.tensor_copy(picked[:], window.indirect(entries))
            for i in range(GROUP):
                tokens[(sort, group * GROUP + i)] = (picked, slice(i * C, (i + 1) * C))

        def interleaved(dst, src, lo, hi):
            return (
                dst[:, lo:hi, :].rearrange("p (c i) j -> p c j i", i=RUN),
                src[:, :, lo:hi].rearrange("p j (c i) -> p c j i", i=RUN),
            )

        def round_on_vector(dst, src, lo, hi):
            to, source = interleaved(dst, src, lo, hi)
            nc.vector.tensor_copy(out=to, in_=source)

        def round_on_scalar(dst, src, lo, hi, e, h):
            to, source = interleaved(dst, src, lo, hi)
            if e < 0:
                nc.scalar.activation(out=to, in_=source, func=IDENT)
            else:
                nc.scalar.activation(out=to, in_=source, func=IDENT, bias=y[h][:, e * C : e * C + 1])

        def quantize(codes, scales, rounded):
            nc.vector.quantize_mx(out=codes.bitcast(FP8X4), scales=scales, in_=rounded)

        def multiply(e, h, codes, scales, width, first, acc):
            token_scales, scale_slots = tokens[(PASSES, e)]
            for o in range(PASSES):
                token_words, word_slots = tokens[(o, e)]
                cols = slice(o * width + first, o * width + first + P)
                nc.tensor.matmul_mx(
                    out=acc,
                    lhsT=codes[:, cols].bitcast(FP8X4),
                    lhsT_scale=scales[:, cols],
                    rhs=token_words[:, word_slots].bitcast(FP8X4),
                    rhs_scale=token_scales[ROWS * o : P, scale_slots],
                    start=(o == 0),
                    stop=(o == PASSES - 1),
                )
            sums[(e, h)] = acc

        def drain(e, h):
            nc.scalar.activation(
                out=y[h][:, e * C : (e + 1) * C], in_=sums[(e, h)], func=IDENT, bias=bias[:, h, e : e + 1]
            )

        def whole_expert(e):
            rounded = ring.tile([P, PASSES, N, PACK], BF16, name="rounded", align_bytes=64)
            codes = ring.tile([P, PASSES * N], U32, name="codes", align_bytes=64)
            scales = ring.tile([P, PASSES * N], U8, name="scales", align_bytes=64)
            cut = N - (VECTOR_COLUMNS_GATHERING if e < GATHERING else VECTOR_COLUMNS_LATER)
            round_on_scalar(rounded[:, 0], raw[(e, 0)], 0, N, e - LAG, 0)
            round_on_scalar(rounded[:, 1], raw[(e, 1)], 0, cut, e - LAG, 1)
            round_on_vector(rounded[:, 1], raw[(e, 1)], cut, N)
            if e >= LAG:
                for h in range(HALVES):
                    drain(e - LAG, h)
            if e < GATHERING:
                gather_tokens(GATHERS - GATHERING + e, f"place{e}")
            quantize(codes[:], scales[:], rounded[:].rearrange("p o n j -> p (o n j)"))
            acc = psum.tile([P, HALVES, C], F32, name="acc", tag="bank")
            for h in range(HALVES):
                multiply(e, h, codes, scales, N, h * P, acc[:, h, :])

        def last_expert_half(h):
            rounded = ring_half.tile([P, PASSES, P, PACK], BF16, name="rounded_half", align_bytes=64)
            codes = ring_half.tile([P, PASSES * P], U32, name="codes_half", align_bytes=64)
            scales = ring_half.tile([P, PASSES * P], U8, name="scales_half", align_bytes=64)
            for o in range(PASSES):
                source = raw[(LAST, o)][:, :, h * P : (h + 1) * P]
                shared = h == 0 and o == PASSES - 1
                cut = P - VECTOR_COLUMNS_LAST if shared else P
                round_on_scalar(rounded[:, o], source, 0, cut, LAST - LAG + o, h)
                if shared:
                    round_on_vector(rounded[:, o], source, cut, P)
                if h == 0:
                    cols = slice(o * P, (o + 1) * P)
                    quantize(codes[:, cols], scales[:, cols], rounded[:, o].rearrange("p n j -> p (n j)"))
            for o in range(PASSES):
                drain(LAST - LAG + o, h)
            if h > 0:
                quantize(codes[:], scales[:], rounded[:].rearrange("p o n j -> p (o n j)"))
            acc = psum.tile([P, C], F32, name="acc_half", tag="bank")
            multiply(LAST, h, codes, scales, P, 0, acc[:])
            drain(LAST, h)

        products = [[keep.tile([P, T], F32, name=f"product{h}{r}") for r in range(TOP)] for h in range(HALVES)]

        for index in range(GATHERS - GATHERING):
            gather_tokens(index, f"picked{index}")
        for e in range(LAST):
            whole_expert(e)
        for h in range(HALVES):
            last_expert_half(h)
        for h in range(HALVES):
            for r in range(TOP):
                nc.vector.tensor_tensor(products[h][r][:], y[h][:].indirect(pos_sb[r][:]), gates[h][r][:], MULT)

        pieces = (slice(0, FIRST_PIECE), slice(FIRST_PIECE, T))
        blocks = [slice(i * P, (i + 1) * P) for i in range(T // P)]

        total = keep.tile([P, T], F32, name="total")
        turned = [psum.tile([P, P], F32, name=f"turned{i}", tag="bank") for i in range(len(blocks))]
        for r in range(TOP):
            for bank, block in zip(turned, blocks):
                nc.tensor.matmul(
                    bank[:],
                    products[0][r][:, block],
                    ident[:],
                    start=(r == 0),
                    stop=(r == TOP - 1),
                    is_transpose=True,
                )
        staged = keep.tile([P, T], F32, name="staged")
        for bank, block in zip(turned, blocks):
            nc.scalar.copy(staged[:, block], bank[:])
        for piece in pieces:
            back = psum.tile([P, piece.stop - piece.start], F32, name="back", tag="bank")
            for block in blocks[piece.start // P : piece.stop // P]:
                nc.tensor.transpose(
                    back[:, block.start - piece.start : block.stop - piece.start], staged[:, block], ident[:]
                )
            nc.scalar.copy(total[:, piece], back[:])
        nc.sync.dma_start(out=out[0:P, :], in_=total[:])

        running = products[1][0]
        for r in range(1, TOP):
            for piece in pieces:
                nc.vector.tensor_tensor(running[:, piece], running[:, piece], products[1][r][:, piece], ADD)
                if r == TOP - 1:
                    nc.sync.dma_start(out=out[P:N, piece], in_=running[:, piece])
